import numpy as np
import ml_dtypes


def mxq(x, axis, fmt="e4m3"):
    dtype, down = {"e4m3": (ml_dtypes.float8_e4m3fn, 7), "e5m2": (ml_dtypes.float8_e5m2, 14)}[fmt]
    v = np.moveaxis(np.asarray(x, np.float32).astype(ml_dtypes.bfloat16).astype(np.float64), axis, -1)
    blocks = v.reshape(v.shape[:-1] + (-1, 32))
    amax = np.abs(blocks).max(-1, keepdims=True)
    byte = np.maximum(np.where(amax > 0, np.frexp(amax)[1] - 1 + 127, 0) - down, 1)
    scale = np.exp2(byte - 127.0)
    codes = (blocks / scale).astype(np.float32).astype(dtype).astype(np.float64)
    return np.moveaxis((codes * scale).reshape(v.shape), -1, axis)


WIDE = False


def mx_kscale(k):
    if not WIDE:
        return np.ones(k)
    levels = np.array([10, -10, 5, -5, 0])
    if k % 512:
        return np.exp2(np.random.permutation(np.resize(levels, k // 32))).repeat(32)
    a = np.empty((k // 512, 16))
    for p in range(k // 512):
        a[p, :8] = np.random.permutation(np.resize(levels, 8))
        for g in range(8):
            far = levels[np.abs(levels - a[p, g]) >= 10]
            a[p, g + 8] = far[np.random.randint(len(far))]
    return np.exp2(a.ravel()).repeat(32)


def f64(x):
    return np.asarray(x).astype(np.float64)


def striped(idx):
    return np.tile(idx.reshape(-1, 16).T, (8, 1)).astype(np.uint16)


def unstriped(offs):
    return offs[:16].T.reshape(-1).astype(np.int64)


E2M1 = np.array([0.0, 0.5, 1.0, 1.5, 2.0, 3.0, 4.0, 6.0, -0.0, -0.5, -1.0, -1.5, -2.0, -3.0, -4.0, -6.0])


def pack_weight(w, fmt):
    k, n = w.shape
    w = f64(np.asarray(w, np.float32).astype(ml_dtypes.bfloat16)).reshape(k // 32, 32, n)
    amax = np.abs(w).max(1)
    if fmt == "e4m3":
        byte = np.frexp(amax)[1] - 1 + 127 - 7
    else:
        mant, ex = np.frexp(amax / 6.0)
        byte = np.where(mant > 0.5, ex, ex - 1) + 127
    byte = np.clip(np.where(amax > 0, byte, 1), 1, 254)
    scaled = (w * np.exp2(127.0 - byte)[:, None, :]).reshape(k, n).astype(np.float32)
    by_word = np.ascontiguousarray(scaled.reshape(k // 512, 128, 4, n).transpose(0, 1, 3, 2))
    if fmt == "e4m3":
        words = by_word.astype(ml_dtypes.float8_e4m3fn).view(np.uint8)
    else:
        c = by_word.astype(ml_dtypes.float4_e2m1fn).view(np.uint8) & 0xF
        words = (c[..., 0::2] | (c[..., 1::2] << 4)).reshape(k // 512, 128, 2 * n)
    return np.ascontiguousarray(words), np.ascontiguousarray(byte.astype(np.uint8).reshape(k // 512, 16, n))


def unpack_weight(words, scales, fmt):
    g, _, n = scales.shape
    words = np.ascontiguousarray(words).reshape(g, 128, n, -1)
    if fmt == "e4m3":
        vals = words.view(ml_dtypes.float8_e4m3fn).astype(np.float64)
    else:
        nib = np.empty((g, 128, n, 4), np.uint8)
        nib[..., 0::2] = words & 0xF
        nib[..., 1::2] = words >> 4
        vals = E2M1[nib]
    vals = vals * np.repeat(np.exp2(scales.astype(np.float64) - 127.0), 8, axis=1)[..., None]
    return vals.transpose(0, 1, 3, 2).reshape(g * 512, n)


def gelu(v):
    return 0.5 * v * (1.0 + np.tanh(np.sqrt(2.0 / np.pi) * (v + 0.044715 * v**3)))


K, T, S, H, T3, S2, T2 = 512, 2048, 1024, 1024, 1024, 512, 2048

def setup_inputs():
    n = np.random.standard_normal
    s = mx_kscale(K)[:, None]
    u = mx_kscale(H)[:, None]
    tab_words, tab_scales = pack_weight(n((K, T)) * s, "e4m3")
    tab2_words, tab2_scales = pack_weight(n((H, T3)) / np.sqrt(H) / u, "e4m3")
    w1_words, w1_scales = pack_weight(0.9 * n((K, H)) / np.sqrt(K) / s * u.T, "e2m1")
    w3_words, w3_scales = pack_weight(1.2 * n((K, H)) / np.sqrt(K) / s * u.T, "e4m3")
    return {
        "tab_words": tab_words, "tab_scales": tab_scales,
        "offs": striped(np.random.permutation(T)[:S]),
        "tab2_words": tab2_words, "tab2_scales": tab2_scales,
        "offs2": striped(np.random.permutation(T3)[:S2]),
        "offs3": striped(np.random.permutation(T2)[:S]),
        "w1_words": w1_words, "w1_scales": w1_scales,
        "w2": (2.0 * n((K, H)) / np.sqrt(K) / s).astype(np.float32),
        "w3_words": w3_words, "w3_scales": w3_scales,
        "gain": (1.5 * np.exp(0.3 * n(H)) * u[:, 0]).astype(np.float32),
        "footing": n((S2, S)).astype(np.float32),
        "pair": np.exp(0.4 * n(S2)).astype(np.float32),
        "page1": (1.5 * n((S2, T2))).astype(np.float32),
        "wgo": np.exp(0.3 * n((128, S))).astype(np.float32),
    }

def reference(tab_words, tab_scales, offs, tab2_words, tab2_scales, offs2, offs3, w1_words, w1_scales, w2, w3_words, w3_scales, gain, footing, pair, page1, wgo):
    v = unpack_weight(tab_words, tab_scales, "e4m3")[:, unstriped(offs)]
    v2 = unpack_weight(tab2_words, tab2_scales, "e4m3")[:, unstriped(offs2)]
    w1 = unpack_weight(w1_words, w1_scales, "e2m1")
    w3 = unpack_weight(w3_words, w3_scales, "e4m3")
    d1 = w1.T @ v
    d2 = mxq(f64(w2), 0, "e4m3").T @ v
    d3 = w3.T @ v
    h = np.maximum(d1 + f64(gain)[:, None] * np.tanh(d2), d3)
    e = v2.T @ mxq(h, 0, "e4m3")
    y = f64(pair)[:, None] * (e + f64(footing))
    out = f64(page1).copy()
    out[:, unstriped(offs3)] = np.tile(f64(wgo), (S2 // 128, 1)) * y
    return out

@@ -1,0 +1,287 @@
+from contextlib import ExitStack
+
+import concourse.mybir as mybir
+from concourse.masks import make_identity
+
+K, T, S, H, T3, S2, T2 = 512, 2048, 1024, 1024, 1024, 512, 2048
+FLOPS = 2 * (3 * K * H * S + H * S2 * S)
+
+F32 = mybir.dt.float32
+BF16 = mybir.dt.bfloat16
+I32 = mybir.dt.int32
+U32 = mybir.dt.uint32
+U16 = mybir.dt.uint16
+U8 = mybir.dt.uint8
+FP8X4 = mybir.dt.float8_e4m3fn_x4
+FP4X4 = mybir.dt.float4_e2m1fn_x4
+ALU = mybir.AluOpType
+ACT = mybir.ActivationFunctionType
+
+P = 128
+PACK = 4
+PASS = P * PACK
+HALF = 512
+QUADS = 4
+N_HALF = S // HALF
+N_PASS = H // PASS
+N_ROWT = S2 // P
+N_COLT = HALF // P
+LIST_COLS = HALF // 16
+
+
+def tile_list_course_fault_page_kernel(
+    tc, tab_words, tab_scales, offs, tab2_words, tab2_scales, offs2, offs3, w1_words, w1_scales, w2,
+    w3_words, w3_scales, gain, footing, pair, page1, wgo, out,
+):
+    nc = tc.nc
+    with ExitStack() as ctx:
+        keep = ctx.enter_context(tc.tile_pool(name="keep", bufs=1))
+        ring = ctx.enter_context(tc.tile_pool(name="ring", bufs=2))
+        psum = ctx.enter_context(tc.psum_pool(name="psum", bufs=2))
+
+        def held(shape, dtype, name):
+            return keep.tile(shape, dtype, name=name, align_bytes=64)
+
+        idx1 = keep.tile([P, S // 16], U16, name="idx1")
+        idx2 = keep.tile([P, S2 // 16], U16, name="idx2")
+        idx3 = keep.tile([P, S // 16], U16, name="idx3")
+        tab_w = held([P, T], I32, "tab_w")
+        tab_s = held([P, T], U8, "tab_s")
+        tab2_w = [held([P, T3], I32, "tab2_w%d" % b) for b in range(N_PASS)]
+        tab2_s = held([P, T3], U8, "tab2_s")
+        w1_raw = held([P, 2 * H], U8, "w1_raw")
+        w3_raw = held([P, H], I32, "w3_raw")
+        ws_raw = held([P, H], U8, "ws_raw")
+        w2_raw = [held([P, PACK, PASS], F32, "w2_raw%d" % b) for b in range(N_PASS)]
+        gain_sb = held([P, N_PASS, PACK], F32, "gain_sb")
+        pair_sb = held([P, N_ROWT], F32, "pair_sb")
+        foot = [held([P, S], F32, "foot%d" % m) for m in range(N_ROWT)]
+        wgo_sb = held([P, S], F32, "wgo_sb")
+        page = [held([P, T2], F32, "page%d" % m) for m in range(N_ROWT)]
+        ident = held([P, P], F32, "ident")
+
+        nc.vector.memset(tab_s[:].bitcast(I32), 0)
+        nc.gpsimd.memset(ws_raw[:].bitcast(I32), 0)
+        nc.gpsimd.memset(tab2_s[:].bitcast(I32), 0)
+
+        def load_scale_rows(queue, tile, first_row, rows):
+            for q in range(QUADS):
+                queue.dma_start(
+                    out=tile[32 * q + first_row : 32 * q + first_row + 4, :].bitcast(I32),
+                    in_=rows[4 * q : 4 * q + 4, :].bitcast(I32),
+                )
+
+        def words(ap):
+            return ap.rearrange("p n i -> p (n i)").bitcast(I32)
+
+        def load_w2(b):
+            nc.sync.dma_start(
+                out=w2_raw[b][:],
+                in_=w2[:, PASS * b : PASS * (b + 1)].rearrange("(p j) c -> p j c", j=PACK),
+            )
+
+        nc.sync.dma_start(idx1[:], offs)
+        load_scale_rows(nc.sync, tab_s, 0, tab_scales[0])
+        load_w2(0)
+        nc.sync.dma_start(out=tab_w[:], in_=words(tab_words[0]))
+        nc.sync.dma_start(out=w1_raw[:].bitcast(I32), in_=w1_words[0].bitcast(I32))
+        load_scale_rows(nc.sync, ws_raw, 0, w1_scales[0])
+        nc.sync.dma_start(out=w3_raw[:], in_=words(w3_words[0]))
+        nc.sync.dma_start(out=gain_sb[:], in_=gain.rearrange("(b p t) -> p b t", b=N_PASS, t=PACK))
+        load_w2(1)
+        for b in range(N_PASS):
+            nc.sync.dma_start(out=tab2_w[b][:], in_=words(tab2_words[b]))
+        nc.sync.dma_start(idx2[:], offs2)
+        for m in range(N_ROWT):
+            nc.sync.dma_start(out=foot[m][:], in_=footing[P * m : P * (m + 1), :])
+        with nc.allow_non_contiguous_dma(reason="one factor a row, one row a partition"):
+            nc.sync.dma_start(out=pair_sb[:], in_=pair.rearrange("(m p) -> p m", p=P))
+        nc.sync.dma_start(idx3[:], offs3)
+        nc.sync.dma_start(out=wgo_sb[:], in_=wgo)
+        for m in range(N_ROWT):
+            nc.sync.dma_start(out=page[m][:], in_=page1[P * m : P * (m + 1), :])
+
+        load_scale_rows(nc.gpsimd, ws_raw, 4, w3_scales[0])
+        for q in range(QUADS):
+            nc.gpsimd.dma_start(
+                out=tab2_s[32 * q : 32 * q + 4 * N_PASS, :].bitcast(I32),
+                in_=tab2_scales[:, 4 * q : 4 * q + 4, :].bitcast(I32),
+            )
+        make_identity(nc, ident[:])
+
+        v_w = [held([P, HALF], U32, "v_w%d" % h) for h in range(N_HALF)]
+        v_s = [held([P, HALF], U8, "v_s%d" % h) for h in range(N_HALF)]
+        v2_w = [held([P, S2], U32, "v2_w%d" % b) for b in range(N_PASS)]
+        v2_s = held([P, S2], U8, "v2_s")
+        w1_p = [held([P, 2 * PASS], U8, "w1_p%d" % b) for b in range(N_PASS)]
+        w3_p = [held([P, PASS], U32, "w3_p%d" % b) for b in range(N_PASS)]
+        ws_p = [held([P, PASS], U8, "ws_p%d" % b) for b in range(N_PASS)]
+        w2_q = [held([P, PASS], U32, "w2_q%d" % b) for b in range(N_PASS)]
+        w2_s = [held([P, PASS], U8, "w2_s%d" % b) for b in range(N_PASS)]
+        w2_g = [held([P, PACK * PASS], BF16, "w2_g%d" % b) for b in range(N_PASS)]
+        h_q = {}
+        h_s = {}
+        h_g = {}
+        foot_t = [held([P, S2], F32, "foot_t%d" % c) for c in range(S // P)]
+
+        def half_list(idx, h):
+            return idx[:, LIST_COLS * h : LIST_COLS * (h + 1)]
+
+        def gather_v_scales(h):
+            nc.vector.tensor_copy(v_s[h][:], tab_s[:].indirect(half_list(idx1, h)))
+
+        def gather_v_words(h):
+            nc.vector.tensor_copy(v_w[h][:], tab_w[:].bitcast(U32).indirect(half_list(idx1, h)))
+
+        def gather_v2_words(b):
+            nc.vector.tensor_copy(v2_w[b][:], tab2_w[b][:].bitcast(U32).indirect(idx2[:]))
+
+        def gather_v2_scales():
+            nc.vector.tensor_copy(v2_s[:], tab2_s[:].indirect(idx2[:]))
+
+        def round_w2(b):
+            nc.scalar.copy(
+                out=w2_g[b][:].rearrange("p (t m j) -> p m j t", t=PACK, j=PACK),
+                in_=w2_raw[b][:].rearrange("p j (m t) -> p m j t", t=PACK),
+            )
+
+        def quantize_w2(b):
+            nc.vector.quantize_mx(out=w2_q[b][:].bitcast(FP8X4), scales=w2_s[b][:], in_=w2_g[b][:])
+
+        def deal(copy, dst, src, run):
+            copy(
+                out=dst.rearrange("p (t c i) -> p c t i", t=PACK, i=run),
+                in_=src.rearrange("p (c i t) -> p c t i", t=PACK, i=run),
+            )
+
+        def deal_weights(b):
+            cols = slice(PASS * b, PASS * (b + 1))
+            deal(nc.scalar.copy, w1_p[b][:].bitcast(U16), w1_raw[:].bitcast(U16)[:, cols], 8)
+            deal(nc.scalar.copy, w3_p[b][:], w3_raw[:].bitcast(U32)[:, cols], 4)
+
+        def deal_scales(b):
+            deal(nc.vector.tensor_copy, ws_p[b][:], ws_raw[:, PASS * b : PASS * (b + 1)], 16)
+
+        def features(h, b):
+            acc = ring.tile([P, PACK, HALF], F32, name="acc")
+            for t in range(PACK):
+                cols = slice(P * t, P * (t + 1))
+                d2 = psum.tile([P, HALF], F32, name="d2")
+                nc.tensor.matmul_mx(
+                    out=d2[:], lhsT=w2_q[b][:, cols].bitcast(FP8X4), lhsT_scale=w2_s[b][:, cols],
+                    rhs=v_w[h][:].bitcast(FP8X4), rhs_scale=v_s[h][:], start=True, stop=True,
+                )
+                d1 = psum.tile([P, HALF], F32, name="d1")
+                nc.tensor.matmul_mx(
+                    out=d1[:], lhsT=w1_p[b][:, 2 * P * t : 2 * P * (t + 1)].bitcast(FP4X4), lhsT_scale=ws_p[b][:, cols],
+                    rhs=v_w[h][:].bitcast(FP8X4), rhs_scale=v_s[h][:], start=True, stop=True,
+                )
+                th = ring.tile([P, HALF], F32, name="th", bufs=3)
+                nc.scalar.activation(out=th[:], in_=d2[:], func=ACT.Tanh)
+                nc.vector.scalar_tensor_tensor(
+                    out=acc[:, t, :], in0=th[:], scalar=gain_sb[:, b, t : t + 1], in1=d1[:], op0=ALU.mult, op1=ALU.add,
+                )
+            h_g[h, b] = ring.tile([P, HALF, PACK], BF16, name="h_g", align_bytes=64)
+            for c in range(N_COLT):
+                js = slice(P * c, P * (c + 1))
+                d3 = psum.tile([P, PACK, P], F32, name="d3")
+                for t in range(PACK):
+                    cols = slice(P * t, P * (t + 1))
+                    nc.tensor.matmul_mx(
+                        out=d3[:, t, :], lhsT=w3_p[b][:, cols].bitcast(FP8X4), lhsT_scale=ws_p[b][4:P, cols],
+                        rhs=v_w[h][:, js].bitcast(FP8X4), rhs_scale=v_s[h][:, js], start=True, stop=True,
+                    )
+                nc.vector.tensor_tensor(
+                    out=h_g[h, b][:, js, :].rearrange("p (u i) t -> p u t i", i=2),
+                    in0=acc[:, :, js].rearrange("p t (u i) -> p u t i", i=2),
+                    in1=d3[:].rearrange("p t (u i) -> p u t i", i=2),
+                    op=ALU.max,
+                )
+            return acc
+
+        def quantize_h(h, b):
+            h_q[h, b] = held([P, HALF], U32, "h_q%d%d" % (h, b))
+            h_s[h, b] = held([P, HALF], U8, "h_s%d%d" % (h, b))
+            nc.vector.quantize_mx(
+                out=h_q[h, b][:].bitcast(FP8X4), scales=h_s[h, b][:], in_=h_g[h, b][:].rearrange("p j t -> p (j t)"),
+            )
+
+        def turn_footing(c):
+            bank = psum.tile([P, S2], F32, name="late")
+            for m in range(N_ROWT):
+                nc.tensor.transpose(bank[:, P * m : P * (m + 1)], foot[m][:, P * c : P * (c + 1)], ident[:])
+            nc.scalar.copy(out=foot_t[c][:], in_=bank[:])
+
+        def products(h):
+            e_t = []
+            for c in range(N_COLT):
+                js = slice(P * c, P * (c + 1))
+                bank = psum.tile([P, S2], F32, name="late")
+                for b in range(N_PASS):
+                    nc.tensor.matmul_mx(
+                        out=bank[:], lhsT=h_q[h, b][:, js].bitcast(FP8X4), lhsT_scale=h_s[h, b][:, js],
+                        rhs=v2_w[b][:].bitcast(FP8X4), rhs_scale=v2_s[4 * b : P, :],
+                        start=(b == 0), stop=(b == N_PASS - 1),
+                    )
+                e_sb = ring.tile([P, S2], F32, name="e_sb", bufs=2 * N_COLT)
+                nc.scalar.copy(out=e_sb[:], in_=bank[:])
+                e_t.append(e_sb)
+            return e_t
+
+        def scores(h, e_t, homes):
+            for m in homes:
+                ms = slice(P * m, P * (m + 1))
+                bank = psum.tile([P, HALF], F32, name="late")
+                for c in range(N_COLT):
+                    js = slice(P * c, P * (c + 1))
+                    nc.tensor.matmul(out=bank[:, js], lhsT=foot_t[N_COLT * h + c][:, ms], rhs=ident[:],
+                                     is_transpose=True, start=True, stop=False)
+                    nc.tensor.matmul(out=bank[:, js], lhsT=e_t[c][:, ms], rhs=ident[:],
+                                     is_transpose=True, start=False, stop=True)
+                nc.scalar.activation(out=homes[m], in_=bank[:], func=ACT.Copy, scale=pair_sb[:, m : m + 1])
+
+        def place(h, m, y):
+            nc.vector.tensor_tensor(
+                out=page[m][:].indirect(half_list(idx3, h)), in0=y, in1=wgo_sb[:, HALF * h : HALF * (h + 1)], op=ALU.mult,
+            )
+
+        gather_v_scales(0)
+        gather_v_scales(1)
+        round_w2(0)
+        deal_scales(0)
+        gather_v_words(0)
+        quantize_w2(0)
+        deal_weights(0)
+        gather_v_words(1)
+        features(0, 0)
+        round_w2(1)
+        deal_weights(1)
+        deal_scales(1)
+        quantize_h(0, 0)
+        features(1, 0)
+        quantize_w2(1)
+        gather_v2_scales()
+        quantize_h(1, 0)
+        for b in range(N_PASS):
+            gather_v2_words(b)
+        for c in range(N_COLT):
+            turn_footing(c)
+        features(0, 1)
+        for c in range(N_COLT, 2 * N_COLT):
+            turn_footing(c)
+        quantize_h(0, 1)
+        e0 = products(0)
+        y0 = {m: held([P, HALF], F32, "y0%d" % m)[:] for m in range(N_ROWT // 2)}
+        scores(0, e0, y0)
+        last_acc = features(1, 1)
+        quantize_h(1, 1)
+        y0_late = {m: last_acc[:, m, :] for m in range(N_ROWT // 2, N_ROWT)}
+        scores(0, e0, y0_late)
+        y0 = {**y0, **y0_late}
+        y1 = {m: held([P, HALF], F32, "y1%d" % m)[:] for m in range(N_ROWT)}
+        scores(1, products(1), y1)
+        for m in range(N_ROWT):
+            place(0, m, y0[m])
+        for m in range(N_ROWT):
+            place(1, m, y1[m])
+            nc.sync.dma_start(out=out[P * m : P * (m + 1), :], in_=page[m][:])

@@ -60,7 +60,6 @@ def tile_list_course_fault_page_kernel(
         page = [held([P, T2], F32, "page%d" % m) for m in range(N_ROWT)]
         ident = held([P, P], F32, "ident")
 
-        nc.vector.memset(tab_s[:].bitcast(I32), 0)
         nc.gpsimd.memset(ws_raw[:].bitcast(I32), 0)
         nc.gpsimd.memset(tab2_s[:].bitcast(I32), 0)
 
@@ -81,9 +80,13 @@ def tile_list_course_fault_page_kernel(
             )
 
         nc.sync.dma_start(idx1[:], offs)
-        load_scale_rows(nc.sync, tab_s, 0, tab_scales[0])
-        load_w2(0)
+        for q in range(QUADS):
+            nc.sync.dma_start(
+                out=tab_s[32 * q : 32 * (q + 1), :].bitcast(I32),
+                in_=tab_scales[0][4 * q : 4 * q + 4, :].bitcast(I32).partition_broadcast(8),
+            )
         nc.sync.dma_start(out=tab_w[:], in_=words(tab_words[0]))
+        load_w2(0)
         nc.sync.dma_start(out=w1_raw[:].bitcast(I32), in_=w1_words[0].bitcast(I32))
         load_scale_rows(nc.sync, ws_raw, 0, w1_scales[0])
         nc.sync.dma_start(out=w3_raw[:], in_=words(w3_words[0]))
@@ -139,11 +142,14 @@ def tile_list_course_fault_page_kernel(
         def gather_v2_scales():
             nc.vector.tensor_copy(v2_s[:], tab2_s[:].indirect(idx2[:]))
 
-        def round_w2(b):
-            nc.scalar.copy(
-                out=w2_g[b][:].rearrange("p (t m j) -> p m j t", t=PACK, j=PACK),
-                in_=w2_raw[b][:].rearrange("p j (m t) -> p m j t", t=PACK),
-            )
+        def round_w2(b, copies):
+            share = P // len(copies)
+            for n, copy in enumerate(copies):
+                ms = slice(share * n, share * (n + 1))
+                copy(
+                    out=w2_g[b][:].rearrange("p (t m j) -> p m j t", t=PACK, j=PACK)[:, ms],
+                    in_=w2_raw[b][:].rearrange("p j (m t) -> p m j t", t=PACK)[:, ms],
+                )
 
         def quantize_w2(b):
             nc.vector.quantize_mx(out=w2_q[b][:].bitcast(FP8X4), scales=w2_s[b][:], in_=w2_g[b][:])
@@ -247,16 +253,16 @@ def tile_list_course_fault_page_kernel(
 
         gather_v_scales(0)
         gather_v_scales(1)
-        round_w2(0)
-        deal_scales(0)
         gather_v_words(0)
+        deal_scales(0)
+        round_w2(0, [nc.scalar.copy, nc.vector.tensor_copy])
         quantize_w2(0)
         deal_weights(0)
         gather_v_words(1)
-        features(0, 0)
-        round_w2(1)
-        deal_weights(1)
         deal_scales(1)
+        features(0, 0)
+        round_w2(1, [nc.scalar.copy, nc.scalar.copy])
+        deal_weights(1)
         quantize_h(0, 0)
         features(1, 0)
         quantize_w2(1)
@@ -264,22 +270,20 @@ def tile_list_course_fault_page_kernel(
         quantize_h(1, 0)
         for b in range(N_PASS):
             gather_v2_words(b)
-        for c in range(N_COLT):
-            turn_footing(c)
         features(0, 1)
-        for c in range(N_COLT, 2 * N_COLT):
+        for c in range(N_COLT):
             turn_footing(c)
         quantize_h(0, 1)
         e0 = products(0)
-        y0 = {m: held([P, HALF], F32, "y0%d" % m)[:] for m in range(N_ROWT // 2)}
-        scores(0, e0, y0)
         last_acc = features(1, 1)
         quantize_h(1, 1)
-        y0_late = {m: last_acc[:, m, :] for m in range(N_ROWT // 2, N_ROWT)}
-        scores(0, e0, y0_late)
-        y0 = {**y0, **y0_late}
+        y0 = {m: last_acc[:, m, :] for m in range(N_ROWT)}
+        scores(0, e0, y0)
+        e1 = products(1)
+        for c in range(N_COLT, 2 * N_COLT):
+            turn_footing(c)
         y1 = {m: held([P, HALF], F32, "y1%d" % m)[:] for m in range(N_ROWT)}
-        scores(1, products(1), y1)
+        scores(1, e1, y1)
         for m in range(N_ROWT):
             place(0, m, y0[m])
         for m in range(N_ROWT):

@@ -37,7 +37,7 @@ def tile_list_course_fault_page_kernel(
     with ExitStack() as ctx:
         keep = ctx.enter_context(tc.tile_pool(name="keep", bufs=1))
         ring = ctx.enter_context(tc.tile_pool(name="ring", bufs=2))
-        psum = ctx.enter_context(tc.psum_pool(name="psum", bufs=2))
+        psum = ctx.enter_context(tc.psum_pool(name="psum", bufs=8))
 
         def held(shape, dtype, name):
             return keep.tile(shape, dtype, name=name, align_bytes=64)
@@ -61,7 +61,6 @@ def tile_list_course_fault_page_kernel(
         ident = held([P, P], F32, "ident")
 
         nc.gpsimd.memset(ws_raw[:].bitcast(I32), 0)
-        nc.gpsimd.memset(tab2_s[:].bitcast(I32), 0)
 
         def load_scale_rows(queue, tile, first_row, rows):
             for q in range(QUADS):
@@ -105,6 +104,7 @@ def tile_list_course_fault_page_kernel(
             nc.sync.dma_start(out=page[m][:], in_=page1[P * m : P * (m + 1), :])
 
         load_scale_rows(nc.gpsimd, ws_raw, 4, w3_scales[0])
+        nc.gpsimd.memset(tab2_s[:].bitcast(I32), 0)
         for q in range(QUADS):
             nc.gpsimd.dma_start(
                 out=tab2_s[32 * q : 32 * q + 4 * N_PASS, :].bitcast(I32),
@@ -125,6 +125,7 @@ def tile_list_course_fault_page_kernel(
         h_q = {}
         h_s = {}
         h_g = {}
+        acc = {}
         foot_t = [held([P, S2], F32, "foot_t%d" % c) for c in range(S // P)]
 
         def half_list(idx, h):
@@ -168,42 +169,46 @@ def tile_list_course_fault_page_kernel(
         def deal_scales(b):
             deal(nc.vector.tensor_copy, ws_p[b][:], ws_raw[:, PASS * b : PASS * (b + 1)], 16)
 
-        def features(h, b):
-            acc = ring.tile([P, PACK, HALF], F32, name="acc")
+        def new_bank():
+            return psum.tile([P, HALF], F32, name="bank")
+
+        def add_gated(h, b, t):
+            if t == 0:
+                acc[h, b] = ring.tile([P, PACK, HALF], F32, name="acc")
+            cols = slice(P * t, P * (t + 1))
+            d2 = new_bank()
+            nc.tensor.matmul_mx(
+                out=d2[:], lhsT=w2_q[b][:, cols].bitcast(FP8X4), lhsT_scale=w2_s[b][:, cols],
+                rhs=v_w[h][:].bitcast(FP8X4), rhs_scale=v_s[h][:], start=True, stop=True,
+            )
+            d1 = new_bank()
+            nc.tensor.matmul_mx(
+                out=d1[:], lhsT=w1_p[b][:, 2 * P * t : 2 * P * (t + 1)].bitcast(FP4X4), lhsT_scale=ws_p[b][:, cols],
+                rhs=v_w[h][:].bitcast(FP8X4), rhs_scale=v_s[h][:], start=True, stop=True,
+            )
+            th = ring.tile([P, HALF], F32, name="th", bufs=PACK)
+            nc.scalar.activation(out=th[:], in_=d2[:], func=ACT.Tanh)
+            nc.vector.scalar_tensor_tensor(
+                out=acc[h, b][:, t, :], in0=th[:], scalar=gain_sb[:, b, t : t + 1], in1=d1[:], op0=ALU.mult, op1=ALU.add,
+            )
+
+        def take_max(h, b, c):
+            if c == 0:
+                h_g[h, b] = ring.tile([P, HALF, PACK], BF16, name="h_g", align_bytes=64)
+            js = slice(P * c, P * (c + 1))
+            d3 = new_bank()
             for t in range(PACK):
                 cols = slice(P * t, P * (t + 1))
-                d2 = psum.tile([P, HALF], F32, name="d2")
                 nc.tensor.matmul_mx(
-                    out=d2[:], lhsT=w2_q[b][:, cols].bitcast(FP8X4), lhsT_scale=w2_s[b][:, cols],
-                    rhs=v_w[h][:].bitcast(FP8X4), rhs_scale=v_s[h][:], start=True, stop=True,
+                    out=d3[:, cols], lhsT=w3_p[b][:, cols].bitcast(FP8X4), lhsT_scale=ws_p[b][4:P, cols],
+                    rhs=v_w[h][:, js].bitcast(FP8X4), rhs_scale=v_s[h][:, js], start=True, stop=True,
                 )
-                d1 = psum.tile([P, HALF], F32, name="d1")
-                nc.tensor.matmul_mx(
-                    out=d1[:], lhsT=w1_p[b][:, 2 * P * t : 2 * P * (t + 1)].bitcast(FP4X4), lhsT_scale=ws_p[b][:, cols],
-                    rhs=v_w[h][:].bitcast(FP8X4), rhs_scale=v_s[h][:], start=True, stop=True,
-                )
-                th = ring.tile([P, HALF], F32, name="th", bufs=3)
-                nc.scalar.activation(out=th[:], in_=d2[:], func=ACT.Tanh)
-                nc.vector.scalar_tensor_tensor(
-                    out=acc[:, t, :], in0=th[:], scalar=gain_sb[:, b, t : t + 1], in1=d1[:], op0=ALU.mult, op1=ALU.add,
-                )
-            h_g[h, b] = ring.tile([P, HALF, PACK], BF16, name="h_g", align_bytes=64)
-            for c in range(N_COLT):
-                js = slice(P * c, P * (c + 1))
-                d3 = psum.tile([P, PACK, P], F32, name="d3")
-                for t in range(PACK):
-                    cols = slice(P * t, P * (t + 1))
-                    nc.tensor.matmul_mx(
-                        out=d3[:, t, :], lhsT=w3_p[b][:, cols].bitcast(FP8X4), lhsT_scale=ws_p[b][4:P, cols],
-                        rhs=v_w[h][:, js].bitcast(FP8X4), rhs_scale=v_s[h][:, js], start=True, stop=True,
-                    )
-                nc.vector.tensor_tensor(
-                    out=h_g[h, b][:, js, :].rearrange("p (u i) t -> p u t i", i=2),
-                    in0=acc[:, :, js].rearrange("p t (u i) -> p u t i", i=2),
-                    in1=d3[:].rearrange("p t (u i) -> p u t i", i=2),
-                    op=ALU.max,
-                )
-            return acc
+            nc.vector.tensor_tensor(
+                out=h_g[h, b][:, js, :].rearrange("p (u i) t -> p u t i", i=2),
+                in0=acc[h, b][:, :, js].rearrange("p t (u i) -> p u t i", i=2),
+                in1=d3[:].rearrange("p (t u i) -> p u t i", t=PACK, i=2),
+                op=ALU.max,
+            )
 
         def quantize_h(h, b):
             h_q[h, b] = held([P, HALF], U32, "h_q%d%d" % (h, b))
@@ -213,31 +218,28 @@ def tile_list_course_fault_page_kernel(
             )
 
         def turn_footing(c):
-            bank = psum.tile([P, S2], F32, name="late")
+            bank = new_bank()
             for m in range(N_ROWT):
                 nc.tensor.transpose(bank[:, P * m : P * (m + 1)], foot[m][:, P * c : P * (c + 1)], ident[:])
             nc.scalar.copy(out=foot_t[c][:], in_=bank[:])
 
-        def products(h):
-            e_t = []
-            for c in range(N_COLT):
-                js = slice(P * c, P * (c + 1))
-                bank = psum.tile([P, S2], F32, name="late")
-                for b in range(N_PASS):
-                    nc.tensor.matmul_mx(
-                        out=bank[:], lhsT=h_q[h, b][:, js].bitcast(FP8X4), lhsT_scale=h_s[h, b][:, js],
-                        rhs=v2_w[b][:].bitcast(FP8X4), rhs_scale=v2_s[4 * b : P, :],
-                        start=(b == 0), stop=(b == N_PASS - 1),
-                    )
-                e_sb = ring.tile([P, S2], F32, name="e_sb", bufs=2 * N_COLT)
-                nc.scalar.copy(out=e_sb[:], in_=bank[:])
-                e_t.append(e_sb)
-            return e_t
+        def product(h, c):
+            js = slice(P * c, P * (c + 1))
+            bank = new_bank()
+            for b in range(N_PASS):
+                nc.tensor.matmul_mx(
+                    out=bank[:], lhsT=h_q[h, b][:, js].bitcast(FP8X4), lhsT_scale=h_s[h, b][:, js],
+                    rhs=v2_w[b][:].bitcast(FP8X4), rhs_scale=v2_s[4 * b : P, :],
+                    start=(b == 0), stop=(b == N_PASS - 1),
+                )
+            e_sb = ring.tile([P, S2], F32, name="e_sb", bufs=2 * N_COLT)
+            nc.scalar.copy(out=e_sb[:], in_=bank[:])
+            return e_sb
 
         def scores(h, e_t, homes):
             for m in homes:
                 ms = slice(P * m, P * (m + 1))
-                bank = psum.tile([P, HALF], F32, name="late")
+                bank = new_bank()
                 for c in range(N_COLT):
                     js = slice(P * c, P * (c + 1))
                     nc.tensor.matmul(out=bank[:, js], lhsT=foot_t[N_COLT * h + c][:, ms], rhs=ident[:],
@@ -259,27 +261,42 @@ def tile_list_course_fault_page_kernel(
         quantize_w2(0)
         deal_weights(0)
         gather_v_words(1)
+        for t in range(PACK):
+            add_gated(0, 0, t)
         deal_scales(1)
-        features(0, 0)
         round_w2(1, [nc.scalar.copy, nc.scalar.copy])
         deal_weights(1)
-        quantize_h(0, 0)
-        features(1, 0)
+        for n in range(PACK):
+            add_gated(1, 0, n)
+            take_max(0, 0, n)
         quantize_w2(1)
-        gather_v2_scales()
-        quantize_h(1, 0)
-        for b in range(N_PASS):
-            gather_v2_words(b)
-        features(0, 1)
+        for n in range(PACK):
+            add_gated(0, 1, n)
+            if n == 0:
+                quantize_h(0, 0)
+            take_max(1, 0, n)
         for c in range(N_COLT):
             turn_footing(c)
+        fillers = [gather_v2_scales, lambda: gather_v2_words(0), lambda: gather_v2_words(1), lambda: add_gated(1, 1, 0)]
+        for c in range(N_COLT):
+            take_max(0, 1, c)
+            if c == 0:
+                quantize_h(1, 0)
+            fillers[c]()
         quantize_h(0, 1)
-        e0 = products(0)
-        last_acc = features(1, 1)
+        for t in range(1, PACK):
+            add_gated(1, 1, t)
+        take_max(1, 1, 0)
+        take_max(1, 1, 1)
+        e0 = [product(0, c) for c in range(3)]
+        take_max(1, 1, 2)
+        e0.append(product(0, 3))
+        take_max(1, 1, 3)
         quantize_h(1, 1)
-        y0 = {m: last_acc[:, m, :] for m in range(N_ROWT)}
-        scores(0, e0, y0)
-        e1 = products(1)
+        y0 = {m: acc[1, 1][:, m, :] for m in range(1, N_ROWT)}
+        y0[0] = held([P, HALF], F32, "y00")[:]
+        scores(0, e0, {m: y0[m] for m in range(N_ROWT)})
+        e1 = [product(1, c) for c in range(N_COLT)]
         for c in range(N_COLT, 2 * N_COLT):
             turn_footing(c)
         y1 = {m: held([P, HALF], F32, "y1%d" % m)[:] for m in range(N_ROWT)}

@@ -84,8 +84,8 @@ def tile_list_course_fault_page_kernel(
                 out=tab_s[32 * q : 32 * (q + 1), :].bitcast(I32),
                 in_=tab_scales[0][4 * q : 4 * q + 4, :].bitcast(I32).partition_broadcast(8),
             )
-        nc.sync.dma_start(out=tab_w[:], in_=words(tab_words[0]))
         load_w2(0)
+        nc.sync.dma_start(out=tab_w[:], in_=words(tab_words[0]))
         nc.sync.dma_start(out=w1_raw[:].bitcast(I32), in_=w1_words[0].bitcast(I32))
         load_scale_rows(nc.sync, ws_raw, 0, w1_scales[0])
         nc.sync.dma_start(out=w3_raw[:], in_=words(w3_words[0]))
@@ -112,7 +112,6 @@ def tile_list_course_fault_page_kernel(
             )
         make_identity(nc, ident[:])
 
-        v_w = [held([P, HALF], U32, "v_w%d" % h) for h in range(N_HALF)]
         v_s = [held([P, HALF], U8, "v_s%d" % h) for h in range(N_HALF)]
         v2_w = [held([P, S2], U32, "v2_w%d" % b) for b in range(N_PASS)]
         v2_s = held([P, S2], U8, "v2_s")
@@ -135,7 +134,7 @@ def tile_list_course_fault_page_kernel(
             nc.vector.tensor_copy(v_s[h][:], tab_s[:].indirect(half_list(idx1, h)))
 
         def gather_v_words(h):
-            nc.vector.tensor_copy(v_w[h][:], tab_w[:].bitcast(U32).indirect(half_list(idx1, h)))
+            nc.vector.tensor_copy(v_w[h], tab_w[:].bitcast(U32).indirect(half_list(idx1, h)))
 
         def gather_v2_words(b):
             nc.vector.tensor_copy(v2_w[b][:], tab2_w[b][:].bitcast(U32).indirect(idx2[:]))
@@ -172,25 +171,35 @@ def tile_list_course_fault_page_kernel(
         def new_bank():
             return psum.tile([P, HALF], F32, name="bank")
 
-        def add_gated(h, b, t):
+        def add_gated(h, b, t, on_gpsimd=False):
             if t == 0:
                 acc[h, b] = ring.tile([P, PACK, HALF], F32, name="acc")
             cols = slice(P * t, P * (t + 1))
             d2 = new_bank()
             nc.tensor.matmul_mx(
                 out=d2[:], lhsT=w2_q[b][:, cols].bitcast(FP8X4), lhsT_scale=w2_s[b][:, cols],
-                rhs=v_w[h][:].bitcast(FP8X4), rhs_scale=v_s[h][:], start=True, stop=True,
+                rhs=v_w[h].bitcast(FP8X4), rhs_scale=v_s[h][:], start=True, stop=True,
             )
             d1 = new_bank()
             nc.tensor.matmul_mx(
                 out=d1[:], lhsT=w1_p[b][:, 2 * P * t : 2 * P * (t + 1)].bitcast(FP4X4), lhsT_scale=ws_p[b][:, cols],
-                rhs=v_w[h][:].bitcast(FP8X4), rhs_scale=v_s[h][:], start=True, stop=True,
+                rhs=v_w[h].bitcast(FP8X4), rhs_scale=v_s[h][:], start=True, stop=True,
             )
             th = ring.tile([P, HALF], F32, name="th", bufs=PACK)
             nc.scalar.activation(out=th[:], in_=d2[:], func=ACT.Tanh)
-            nc.vector.scalar_tensor_tensor(
-                out=acc[h, b][:, t, :], in0=th[:], scalar=gain_sb[:, b, t : t + 1], in1=d1[:], op0=ALU.mult, op1=ALU.add,
-            )
+            if on_gpsimd:
+                d1_sb = ring.tile([P, HALF], F32, name="d1_sb")
+                nc.scalar.copy(out=d1_sb[:], in_=d1[:])
+                gated = ring.tile([P, HALF], F32, name="gated")
+                nc.gpsimd.tensor_scalar(
+                    out=gated[:], in0=th[:], scalar1=gain_sb[:, b, t : t + 1], scalar2=0.0, op0=ALU.mult, op1=ALU.add,
+                )
+                nc.gpsimd.tensor_tensor(out=acc[h, b][:, t, :], in0=gated[:], in1=d1_sb[:], op=ALU.add)
+            else:
+                nc.vector.scalar_tensor_tensor(
+                    out=acc[h, b][:, t, :], in0=th[:], scalar=gain_sb[:, b, t : t + 1], in1=d1[:],
+                    op0=ALU.mult, op1=ALU.add,
+                )
 
         def take_max(h, b, c):
             if c == 0:
@@ -255,10 +264,12 @@ def tile_list_course_fault_page_kernel(
 
         gather_v_scales(0)
         gather_v_scales(1)
-        gather_v_words(0)
-        deal_scales(0)
         round_w2(0, [nc.scalar.copy, nc.vector.tensor_copy])
         quantize_w2(0)
+        v_words = keep.tile([P, S], U32, name="v_words", tag="w2_g0", align_bytes=64)
+        v_w = [v_words[:, HALF * h : HALF * (h + 1)] for h in range(N_HALF)]
+        gather_v_words(0)
+        deal_scales(0)
         deal_weights(0)
         gather_v_words(1)
         for t in range(PACK):
@@ -266,15 +277,20 @@ def tile_list_course_fault_page_kernel(
         deal_scales(1)
         round_w2(1, [nc.scalar.copy, nc.scalar.copy])
         deal_weights(1)
-        for n in range(PACK):
+        add_gated(1, 0, 0, True)
+        for n in range(1, PACK):
             add_gated(1, 0, n)
-            take_max(0, 0, n)
+            take_max(0, 0, n - 1)
         quantize_w2(1)
-        for n in range(PACK):
+        take_max(0, 0, PACK - 1)
+        add_gated(0, 1, 0, True)
+        add_gated(0, 1, 1, True)
+        take_max(1, 0, 0)
+        quantize_h(0, 0)
+        for n in range(2, PACK):
             add_gated(0, 1, n)
-            if n == 0:
-                quantize_h(0, 0)
-            take_max(1, 0, n)
+            take_max(1, 0, n - 1)
+        take_max(1, 0, PACK - 1)
         for c in range(N_COLT):
             turn_footing(c)
         fillers = [gather_v2_scales, lambda: gather_v2_words(0), lambda: gather_v2_words(1), lambda: add_gated(1, 1, 0)]

from contextlib import ExitStack

import concourse.mybir as mybir
from concourse.masks import make_identity

K, T, S, H, T3, S2, T2 = 512, 2048, 1024, 1024, 1024, 512, 2048
FLOPS = 2 * (3 * K * H * S + H * S2 * S)

F32 = mybir.dt.float32
BF16 = mybir.dt.bfloat16
I32 = mybir.dt.int32
U32 = mybir.dt.uint32
U16 = mybir.dt.uint16
U8 = mybir.dt.uint8
FP8X4 = mybir.dt.float8_e4m3fn_x4
FP4X4 = mybir.dt.float4_e2m1fn_x4
ALU = mybir.AluOpType
ACT = mybir.ActivationFunctionType

P = 128
PACK = 4
PASS = P * PACK
HALF = 512
QUADS = 4
N_HALF = S // HALF
N_PASS = H // PASS
N_ROWT = S2 // P
N_COLT = HALF // P
LIST_COLS = HALF // 16


def tile_list_course_fault_page_kernel(
    tc, tab_words, tab_scales, offs, tab2_words, tab2_scales, offs2, offs3, w1_words, w1_scales, w2,
    w3_words, w3_scales, gain, footing, pair, page1, wgo, out,
):
    nc = tc.nc
    with ExitStack() as ctx:
        keep = ctx.enter_context(tc.tile_pool(name="keep", bufs=1))
        ring = ctx.enter_context(tc.tile_pool(name="ring", bufs=2))
        psum = ctx.enter_context(tc.psum_pool(name="psum", bufs=8))

        def held(shape, dtype, name):
            return keep.tile(shape, dtype, name=name, align_bytes=64)

        idx1 = keep.tile([P, S // 16], U16, name="idx1")
        idx2 = keep.tile([P, S2 // 16], U16, name="idx2")
        idx3 = keep.tile([P, S // 16], U16, name="idx3")
        tab_w = held([P, T], I32, "tab_w")
        tab_s = held([P, T], U8, "tab_s")
        tab2_w = [held([P, T3], I32, "tab2_w%d" % b) for b in range(N_PASS)]
        tab2_s = held([P, T3], U8, "tab2_s")
        w1_raw = held([P, 2 * H], U8, "w1_raw")
        w3_raw = held([P, H], I32, "w3_raw")
        ws_raw = held([P, H], U8, "ws_raw")
        w2_raw = [held([P, PACK, PASS], F32, "w2_raw%d" % b) for b in range(N_PASS)]
        gain_sb = held([P, N_PASS, PACK], F32, "gain_sb")
        pair_sb = held([P, N_ROWT], F32, "pair_sb")
        foot = [held([P, S], F32, "foot%d" % m) for m in range(N_ROWT)]
        wgo_sb = held([P, S], F32, "wgo_sb")
        page = [held([P, T2], F32, "page%d" % m) for m in range(N_ROWT)]
        ident = held([P, P], F32, "ident")

        nc.gpsimd.memset(ws_raw[:].bitcast(I32), 0)

        def load_scale_rows(queue, tile, first_row, rows):
            for q in range(QUADS):
                queue.dma_start(
                    out=tile[32 * q + first_row : 32 * q + first_row + 4, :].bitcast(I32),
                    in_=rows[4 * q : 4 * q + 4, :].bitcast(I32),
                )

        def words(ap):
            return ap.rearrange("p n i -> p (n i)").bitcast(I32)

        def load_w2(b):
            nc.sync.dma_start(
                out=w2_raw[b][:],
                in_=w2[:, PASS * b : PASS * (b + 1)].rearrange("(p j) c -> p j c", j=PACK),
            )

        nc.sync.dma_start(idx1[:], offs)
        for q in range(QUADS):
            nc.sync.dma_start(
                out=tab_s[32 * q : 32 * (q + 1), :].bitcast(I32),
                in_=tab_scales[0][4 * q : 4 * q + 4, :].bitcast(I32).partition_broadcast(8),
            )
        load_w2(0)
        nc.sync.dma_start(out=tab_w[:], in_=words(tab_words[0]))
        nc.sync.dma_start(out=w1_raw[:].bitcast(I32), in_=w1_words[0].bitcast(I32))
        load_scale_rows(nc.sync, ws_raw, 0, w1_scales[0])
        nc.sync.dma_start(out=w3_raw[:], in_=words(w3_words[0]))
        nc.sync.dma_start(out=gain_sb[:], in_=gain.rearrange("(b p t) -> p b t", b=N_PASS, t=PACK))
        load_w2(1)
        for b in range(N_PASS):
            nc.sync.dma_start(out=tab2_w[b][:], in_=words(tab2_words[b]))
        nc.sync.dma_start(idx2[:], offs2)
        for m in range(N_ROWT):
            nc.sync.dma_start(out=foot[m][:], in_=footing[P * m : P * (m + 1), :])
        with nc.allow_non_contiguous_dma(reason="one factor a row, one row a partition"):
            nc.sync.dma_start(out=pair_sb[:], in_=pair.rearrange("(m p) -> p m", p=P))
        nc.sync.dma_start(idx3[:], offs3)
        nc.sync.dma_start(out=wgo_sb[:], in_=wgo)
        for m in range(N_ROWT):
            nc.sync.dma_start(out=page[m][:], in_=page1[P * m : P * (m + 1), :])

        load_scale_rows(nc.gpsimd, ws_raw, 4, w3_scales[0])
        nc.gpsimd.memset(tab2_s[:].bitcast(I32), 0)
        for q in range(QUADS):
            nc.gpsimd.dma_start(
                out=tab2_s[32 * q : 32 * q + 4 * N_PASS, :].bitcast(I32),
                in_=tab2_scales[:, 4 * q : 4 * q + 4, :].bitcast(I32),
            )
        make_identity(nc, ident[:])

        v_s = [held([P, HALF], U8, "v_s%d" % h) for h in range(N_HALF)]
        v2_w = [held([P, S2], U32, "v2_w%d" % b) for b in range(N_PASS)]
        v2_s = held([P, S2], U8, "v2_s")
        w1_p = [held([P, 2 * PASS], U8, "w1_p%d" % b) for b in range(N_PASS)]
        w3_p = [held([P, PASS], U32, "w3_p%d" % b) for b in range(N_PASS)]
        ws_p = [held([P, PASS], U8, "ws_p%d" % b) for b in range(N_PASS)]
        w2_q = [held([P, PASS], U32, "w2_q%d" % b) for b in range(N_PASS)]
        w2_s = [held([P, PASS], U8, "w2_s%d" % b) for b in range(N_PASS)]
        w2_g = [held([P, PACK * PASS], BF16, "w2_g%d" % b) for b in range(N_PASS)]
        h_q = {}
        h_s = {}
        h_g = {}
        acc = {}
        foot_t = [held([P, S2], F32, "foot_t%d" % c) for c in range(S // P)]

        def half_list(idx, h):
            return idx[:, LIST_COLS * h : LIST_COLS * (h + 1)]

        def gather_v_scales(h):
            nc.vector.tensor_copy(v_s[h][:], tab_s[:].indirect(half_list(idx1, h)))

        def gather_v_words(h):
            nc.vector.tensor_copy(v_w[h], tab_w[:].bitcast(U32).indirect(half_list(idx1, h)))

        def gather_v2_words(b):
            nc.vector.tensor_copy(v2_w[b][:], tab2_w[b][:].bitcast(U32).indirect(idx2[:]))

        def gather_v2_scales():
            nc.vector.tensor_copy(v2_s[:], tab2_s[:].indirect(idx2[:]))

        def round_w2(b, copies):
            share = P // len(copies)
            for n, copy in enumerate(copies):
                ms = slice(share * n, share * (n + 1))
                copy(
                    out=w2_g[b][:].rearrange("p (t m j) -> p m j t", t=PACK, j=PACK)[:, ms],
                    in_=w2_raw[b][:].rearrange("p j (m t) -> p m j t", t=PACK)[:, ms],
                )

        def quantize_w2(b):
            nc.vector.quantize_mx(out=w2_q[b][:].bitcast(FP8X4), scales=w2_s[b][:], in_=w2_g[b][:])

        def deal(copy, dst, src, run):
            copy(
                out=dst.rearrange("p (t c i) -> p c t i", t=PACK, i=run),
                in_=src.rearrange("p (c i t) -> p c t i", t=PACK, i=run),
            )

        def deal_weights(b):
            cols = slice(PASS * b, PASS * (b + 1))
            deal(nc.scalar.copy, w1_p[b][:].bitcast(U16), w1_raw[:].bitcast(U16)[:, cols], 8)
            deal(nc.scalar.copy, w3_p[b][:], w3_raw[:].bitcast(U32)[:, cols], 4)

        def deal_scales(b):
            deal(nc.vector.tensor_copy, ws_p[b][:], ws_raw[:, PASS * b : PASS * (b + 1)], 16)

        def new_bank():
            return psum.tile([P, HALF], F32, name="bank")

        def add_gated(h, b, t, on_gpsimd=False):
            if t == 0:
                acc[h, b] = ring.tile([P, PACK, HALF], F32, name="acc")
            cols = slice(P * t, P * (t + 1))
            d2 = new_bank()
            nc.tensor.matmul_mx(
                out=d2[:], lhsT=w2_q[b][:, cols].bitcast(FP8X4), lhsT_scale=w2_s[b][:, cols],
                rhs=v_w[h].bitcast(FP8X4), rhs_scale=v_s[h][:], start=True, stop=True,
            )
            d1 = new_bank()
            nc.tensor.matmul_mx(
                out=d1[:], lhsT=w1_p[b][:, 2 * P * t : 2 * P * (t + 1)].bitcast(FP4X4), lhsT_scale=ws_p[b][:, cols],
                rhs=v_w[h].bitcast(FP8X4), rhs_scale=v_s[h][:], start=True, stop=True,
            )
            th = ring.tile([P, HALF], F32, name="th", bufs=PACK)
            nc.scalar.activation(out=th[:], in_=d2[:], func=ACT.Tanh)
            if on_gpsimd:
                d1_sb = ring.tile([P, HALF], F32, name="d1_sb")
                nc.scalar.copy(out=d1_sb[:], in_=d1[:])
                gated = ring.tile([P, HALF], F32, name="gated")
                nc.gpsimd.tensor_scalar(
                    out=gated[:], in0=th[:], scalar1=gain_sb[:, b, t : t + 1], scalar2=0.0, op0=ALU.mult, op1=ALU.add,
                )
                nc.gpsimd.tensor_tensor(out=acc[h, b][:, t, :], in0=gated[:], in1=d1_sb[:], op=ALU.add)
            else:
                nc.vector.scalar_tensor_tensor(
                    out=acc[h, b][:, t, :], in0=th[:], scalar=gain_sb[:, b, t : t + 1], in1=d1[:],
                    op0=ALU.mult, op1=ALU.add,
                )

        def take_max(h, b, c):
            if c == 0:
                h_g[h, b] = ring.tile([P, HALF, PACK], BF16, name="h_g", align_bytes=64)
            js = slice(P * c, P * (c + 1))
            d3 = new_bank()
            for t in range(PACK):
                cols = slice(P * t, P * (t + 1))
                nc.tensor.matmul_mx(
                    out=d3[:, cols], lhsT=w3_p[b][:, cols].bitcast(FP8X4), lhsT_scale=ws_p[b][4:P, cols],
                    rhs=v_w[h][:, js].bitcast(FP8X4), rhs_scale=v_s[h][:, js], start=True, stop=True,
                )
            nc.vector.tensor_tensor(
                out=h_g[h, b][:, js, :].rearrange("p (u i) t -> p u t i", i=2),
                in0=acc[h, b][:, :, js].rearrange("p t (u i) -> p u t i", i=2),
                in1=d3[:].rearrange("p (t u i) -> p u t i", t=PACK, i=2),
                op=ALU.max,
            )

        def quantize_h(h, b):
            h_q[h, b] = held([P, HALF], U32, "h_q%d%d" % (h, b))
            h_s[h, b] = held([P, HALF], U8, "h_s%d%d" % (h, b))
            nc.vector.quantize_mx(
                out=h_q[h, b][:].bitcast(FP8X4), scales=h_s[h, b][:], in_=h_g[h, b][:].rearrange("p j t -> p (j t)"),
            )

        def turn_footing(c):
            bank = new_bank()
            for m in range(N_ROWT):
                nc.tensor.transpose(bank[:, P * m : P * (m + 1)], foot[m][:, P * c : P * (c + 1)], ident[:])
            nc.scalar.copy(out=foot_t[c][:], in_=bank[:])

        def product(h, c):
            js = slice(P * c, P * (c + 1))
            bank = new_bank()
            for b in range(N_PASS):
                nc.tensor.matmul_mx(
                    out=bank[:], lhsT=h_q[h, b][:, js].bitcast(FP8X4), lhsT_scale=h_s[h, b][:, js],
                    rhs=v2_w[b][:].bitcast(FP8X4), rhs_scale=v2_s[4 * b : P, :],
                    start=(b == 0), stop=(b == N_PASS - 1),
                )
            e_sb = ring.tile([P, S2], F32, name="e_sb", bufs=2 * N_COLT)
            nc.scalar.copy(out=e_sb[:], in_=bank[:])
            return e_sb

        def scores(h, e_t, homes):
            for m in homes:
                ms = slice(P * m, P * (m + 1))
                bank = new_bank()
                for c in range(N_COLT):
                    js = slice(P * c, P * (c + 1))
                    nc.tensor.matmul(out=bank[:, js], lhsT=foot_t[N_COLT * h + c][:, ms], rhs=ident[:],
                                     is_transpose=True, start=True, stop=False)
                    nc.tensor.matmul(out=bank[:, js], lhsT=e_t[c][:, ms], rhs=ident[:],
                                     is_transpose=True, start=False, stop=True)
                nc.scalar.activation(out=homes[m], in_=bank[:], func=ACT.Copy, scale=pair_sb[:, m : m + 1])

        def place(h, m, y):
            nc.vector.tensor_tensor(
                out=page[m][:].indirect(half_list(idx3, h)), in0=y, in1=wgo_sb[:, HALF * h : HALF * (h + 1)], op=ALU.mult,
            )

        gather_v_scales(0)
        gather_v_scales(1)
        round_w2(0, [nc.scalar.copy, nc.vector.tensor_copy])
        quantize_w2(0)
        v_words = keep.tile([P, S], U32, name="v_words", tag="w2_g0", align_bytes=64)
        v_w = [v_words[:, HALF * h : HALF * (h + 1)] for h in range(N_HALF)]
        gather_v_words(0)
        deal_scales(0)
        deal_weights(0)
        gather_v_words(1)
        for t in range(PACK):
            add_gated(0, 0, t)
        deal_scales(1)
        round_w2(1, [nc.scalar.copy, nc.scalar.copy])
        deal_weights(1)
        add_gated(1, 0, 0, True)
        for n in range(1, PACK):
            add_gated(1, 0, n)
            take_max(0, 0, n - 1)
        quantize_w2(1)
        take_max(0, 0, PACK - 1)
        add_gated(0, 1, 0, True)
        add_gated(0, 1, 1, True)
        take_max(1, 0, 0)
        quantize_h(0, 0)
        for n in range(2, PACK):
            add_gated(0, 1, n)
            take_max(1, 0, n - 1)
        take_max(1, 0, PACK - 1)
        for c in range(N_COLT):
            turn_footing(c)
        fillers = [gather_v2_scales, lambda: gather_v2_words(0), lambda: gather_v2_words(1), lambda: add_gated(1, 1, 0)]
        for c in range(N_COLT):
            take_max(0, 1, c)
            if c == 0:
                quantize_h(1, 0)
            fillers[c]()
        quantize_h(0, 1)
        for t in range(1, PACK):
            add_gated(1, 1, t)
        take_max(1, 1, 0)
        take_max(1, 1, 1)
        e0 = [product(0, c) for c in range(3)]
        take_max(1, 1, 2)
        e0.append(product(0, 3))
        take_max(1, 1, 3)
        quantize_h(1, 1)
        y0 = {m: acc[1, 1][:, m, :] for m in range(1, N_ROWT)}
        y0[0] = held([P, HALF], F32, "y00")[:]
        scores(0, e0, {m: y0[m] for m in range(N_ROWT)})
        e1 = [product(1, c) for c in range(N_COLT)]
        for c in range(N_COLT, 2 * N_COLT):
            turn_footing(c)
        y1 = {m: held([P, HALF], F32, "y1%d" % m)[:] for m in range(N_ROWT)}
        scores(1, e1, y1)
        for m in range(N_ROWT):
            place(0, m, y0[m])
        for m in range(N_ROWT):
            place(1, m, y1[m])
            nc.sync.dma_start(out=out[P * m : P * (m + 1), :], in_=page[m][:])
